import numpy as np
import ml_dtypes


def mxq(x, axis, fmt="e4m3"):
    dtype, down = {"e4m3": (ml_dtypes.float8_e4m3fn, 7), "e5m2": (ml_dtypes.float8_e5m2, 14)}[fmt]
    v = np.moveaxis(np.asarray(x, np.float32).astype(ml_dtypes.bfloat16).astype(np.float64), axis, -1)
    blocks = v.reshape(v.shape[:-1] + (-1, 32))
    amax = np.abs(blocks).max(-1, keepdims=True)
    byte = np.maximum(np.where(amax > 0, np.frexp(amax)[1] - 1 + 127, 0) - down, 1)
    scale = np.exp2(byte - 127.0)
    codes = (blocks / scale).astype(np.float32).astype(dtype).astype(np.float64)
    return np.moveaxis((codes * scale).reshape(v.shape), -1, axis)


WIDE = False


def mx_kscale(k):
    if not WIDE:
        return np.ones(k)
    levels = np.array([10, -10, 5, -5, 0])
    if k % 512:
        return np.exp2(np.random.permutation(np.resize(levels, k // 32))).repeat(32)
    a = np.empty((k // 512, 16))
    for p in range(k // 512):
        a[p, :8] = np.random.permutation(np.resize(levels, 8))
        for g in range(8):
            far = levels[np.abs(levels - a[p, g]) >= 10]
            a[p, g + 8] = far[np.random.randint(len(far))]
    return np.exp2(a.ravel()).repeat(32)


def f64(x):
    return np.asarray(x).astype(np.float64)


def striped(idx):
    return np.tile(np.asarray(idx).reshape(-1, 16).T, (8, 1)).astype(np.uint16)


def unstriped(offs):
    return offs[:16].T.reshape(-1).astype(np.int64)


def bf(x):
    return np.asarray(x, np.float32).astype(ml_dtypes.bfloat16)


def planes(Y):
    r, m = Y.shape
    b = f64(bf(Y)).reshape(r // 32, 32, m)
    amax = np.abs(b).max(1)
    byte = np.clip(np.where(amax > 0, np.frexp(amax)[1] - 1 + 127 - 7, 1), 1, 254)
    codes = (b * np.exp2(127.0 - byte)[:, None, :]).reshape(r, m).astype(np.float32).astype(ml_dtypes.float8_e4m3fn).view(np.uint8)
    words = codes.reshape(r // 512, 128, 4, m).transpose(0, 1, 3, 2)
    return np.ascontiguousarray(words), np.ascontiguousarray(byte.astype(np.uint8).reshape(r // 512, 16, m))


D, T, I, E = 512, 2048, 512, 512


def setup_inputs():
    n = np.random.standard_normal
    idx = np.random.permutation(T)[:I]
    fd = mx_kscale(D)
    fi = mx_kscale(I)
    return {
        "state": (n((D, E)) * 1 / np.sqrt(D) * fd[:, None]).astype(np.float32),
        "keys": (n((D, T)) / fd[:, None]).astype(np.float32),
        "vals": (n((E, T))).astype(np.float32),
        "step": (np.random.uniform(0.05, 0.2, (I, 1)) * fi[:, None]).astype(np.float32),
        "vsc": (np.random.uniform(0.5, 2.0, (I, 1)) / fi[:, None]).astype(np.float32),
        "dsc": (np.random.uniform(0.5, 2.0, (1, D)) * fd).astype(np.float32),
        "offs": striped(idx),
    }


def reference(state, keys, vals, step, vsc, dsc, offs):
    idx = unstriped(offs)
    stateq = mxq(f64(state), 0, "e4m3")
    keysidxq = mxq(f64(keys)[:, idx], 0, "e4m3")
    b = stateq.T @ keysidxq
    err = f64(vals)[:, idx] - b
    et = err.T
    es = et * f64(vsc)
    kt = f64(keys)[:, idx].T
    ks = kt * f64(step) * f64(dsc)
    ksq = mxq(ks, 0, "e4m3")
    esq = mxq(es, 0, "e4m3")
    y = ksq.T @ esq
    words, scales = planes(y)
    return y, words, scales

@@ -1,0 +1,239 @@
+from contextlib import ExitStack
+
+import concourse.mybir as mybir
+from concourse.masks import make_identity
+
+D, T, I, E = 512, 2048, 512, 512
+FLOPS = 2 * D * I * E + 2 * I * D * E
+
+F32 = mybir.dt.float32
+BF16 = mybir.dt.bfloat16
+I32 = mybir.dt.int32
+U32 = mybir.dt.uint32
+U16 = mybir.dt.uint16
+U8 = mybir.dt.uint8
+FP8X4 = mybir.dt.float8_e4m3fn_x4
+MULT = mybir.AluOpType.mult
+COPY = mybir.ActivationFunctionType.Copy
+
+P = 128
+PACK = 4
+WINDOW_BYTES = 4 * T
+KEY_CAST_ON_VECTOR = 256
+
+
+def block(j, n=1):
+    return slice(j * P, (j + n) * P)
+
+
+def tile_attend_deltastep_pl_kernel(tc, state, keys, vals, step, vsc, dsc, offs, out_0, out_1, out_2):
+    nc = tc.nc
+    with ExitStack() as ctx:
+        keep = ctx.enter_context(tc.tile_pool(name="keep", bufs=1))
+        windows = ctx.enter_context(tc.tile_pool(name="windows", bufs=1))
+        psum = ctx.enter_context(tc.psum_pool(name="psum", bufs=1))
+
+        def on_window(w, at, shape, dtype, name):
+            return windows.tile(shape, dtype, name=name, offset=w * WINDOW_BYTES + at, align_bytes=64)
+
+        offsets = keep.tile([P, I // 16], U16, name="offsets")
+        key_pool = [on_window(t, 0, [P, T], F32, "key_pool%d" % t) for t in range(PACK)]
+        val_pool = [on_window(PACK + j, 0, [P, T], F32, "val_pool%d" % j) for j in range(E // P)]
+        state_raw = keep.tile([P, PACK, E], F32, name="state_raw")
+        dsc_sb = keep.tile([P, PACK], F32, name="dsc_sb")
+        step_sb = keep.tile([P, PACK], F32, name="step_sb")
+        vsc_sb = keep.tile([P, PACK], F32, name="vsc_sb")
+        ident = keep.tile([P, P], F32, name="ident")
+
+        key_planes = keys.rearrange("(p t) n -> p t n", t=PACK)
+        nc.sync.dma_start(key_pool[0][:], key_planes[:, 0, :])
+        nc.sync.dma_start(offsets[:], offs)
+        nc.scalar.dma_start(dsc_sb[:], dsc.rearrange("o (p t) -> p (o t)", t=PACK))
+        nc.scalar.dma_start(step_sb[:], step.rearrange("(s r) o -> s (r o)", r=PACK))
+        nc.scalar.dma_start(vsc_sb[:], vsc.rearrange("(s r) o -> s (r o)", r=PACK))
+        for t in range(1, PACK):
+            nc.sync.dma_start(key_pool[t][:], key_planes[:, t, :])
+        nc.sync.dma_start(state_raw[:], state.rearrange("(p t) e -> p t e", t=PACK))
+        for j in range(E // P):
+            nc.sync.dma_start(val_pool[j][:], vals[block(j), :])
+        make_identity(nc, ident[:])
+
+        def gather_dealt(dst, window):
+            nc.vector.tensor_copy(
+                out=dst.bitcast(U32).rearrange("p (r s) -> p s r", r=PACK),
+                in_=window[:].bitcast(U32).indirect(offsets[:]),
+            )
+
+        def quantize(codes, scales, grouped):
+            nc.vector.quantize_mx(out=codes.bitcast(FP8X4), scales=scales, in_=grouped.rearrange("p c t -> p (c t)"))
+
+        def per_slot(scale_sb):
+            return scale_sb[:].unsqueeze(1).to_broadcast([P, P, PACK])
+
+        def interleaved(dst, src):
+            return (
+                dst.rearrange("p (c i) t -> p c t i", i=4),
+                src.rearrange("p t (c i) -> p c t i", i=4),
+            )
+
+        def turn_into(bank, src, start, stop):
+            for r in range(PACK):
+                nc.tensor.matmul(
+                    bank[:, r, :],
+                    src[:, block(r)],
+                    ident[:],
+                    start=start and r == 0,
+                    stop=stop and r == PACK - 1,
+                    is_transpose=True,
+                )
+
+        listed_keys = keep.tile([P, PACK, I], F32, name="listed_keys")
+        ks_codes = keep.tile([P, D], U32, name="ks_codes", align_bytes=64)
+        ks_scales = keep.tile([P, D], U8, name="ks_scales", align_bytes=64)
+        key_bf = keep.tile([P, I, PACK], BF16, name="key_bf", align_bytes=64)
+        key_codes = keep.tile([P, I], U32, name="key_codes", align_bytes=64)
+        key_scales = keep.tile([P, I], U8, name="key_scales", align_bytes=64)
+        state_bf = keep.tile([P, E, PACK], BF16, name="state_bf", align_bytes=64)
+        state_scales = keep.tile([P, E], U8, name="state_scales", align_bytes=64)
+        es_codes = keep.tile([P, E], U32, name="es_codes", align_bytes=64)
+        es_scales = keep.tile([P, E], U8, name="es_scales", align_bytes=64)
+        y_bf = keep.tile([P, E, PACK], BF16, name="y_bf", align_bytes=64)
+        y_scales = keep.tile([P, E], U8, name="y_scales", align_bytes=64)
+        y_rows = out_0.rearrange("(p t) e -> p t e", t=PACK)
+        word_rows = out_1.rearrange("z p c r -> p (z c r)").bitcast(I32)
+        scale_rows = out_2.rearrange("z q c -> q (z c)").bitcast(I32)
+
+        def turn_keys(t):
+            kd = keep.tile([P, I], F32, name="kd%d" % t)
+            nc.scalar.activation(out=kd[:], in_=listed_keys[:, t, :], func=COPY, scale=dsc_sb[:, t : t + 1])
+            turned = psum.tile([P, PACK, P], F32, name="turned", tag="work", bufs=2)
+            turn_into(turned, kd, True, True)
+            return turned
+
+        def scale_ks(turned, ks_bf):
+            nc.vector.tensor_tensor(out=ks_bf, in0=turned[:].rearrange("s r p -> s p r"), in1=per_slot(step_sb), op=MULT)
+
+        def quantize_ks(t, n, ks_bf):
+            quantize(ks_codes[:, block(t, n)], ks_scales[:, block(t, n)], ks_bf)
+
+        def gather_vals(j):
+            listed_vals = keep.tile([P, I], F32, name="listed_vals%d" % j)
+            gather_dealt(listed_vals[:], val_pool[j])
+            return listed_vals
+
+        def cast_state(j, n):
+            cols = block(j, n)
+            nc.scalar.copy(*interleaved(state_bf[:, cols, :], state_raw[:, :, cols]))
+
+        def quantize_state(j, n, codes):
+            cols = block(j, n)
+            quantize(codes, state_scales[:, cols], state_bf[:, cols, :])
+
+        def predict(j, codes):
+            b = psum.tile([P, I], F32, name="b", tag="work", bufs=2)
+            nc.tensor.matmul_mx(
+                out=b[:],
+                lhsT=codes[:, block(j % 2)].bitcast(FP8X4),
+                lhsT_scale=state_scales[:, block(j)],
+                rhs=key_codes[:].bitcast(FP8X4),
+                rhs_scale=key_scales[:],
+                start=True,
+                stop=True,
+            )
+            minus_b = keep.tile([P, I], F32, name="minus_b%d" % j)
+            nc.scalar.activation(out=minus_b[:], in_=b[:], func=COPY, scale=-1.0)
+            return minus_b
+
+        def make_es(j, err, es_bf):
+            nc.vector.tensor_tensor(out=es_bf[:], in0=err[:].rearrange("s r e -> s e r"), in1=per_slot(vsc_sb), op=MULT)
+            quantize(es_codes[:, block(j)], es_scales[:, block(j)], es_bf[:])
+
+        def update(j):
+            y = psum.tile([P, PACK, P], F32, name="y", tag="y", bufs=2)
+            for t in range(PACK):
+                nc.tensor.matmul_mx(
+                    out=y[:, t, :],
+                    lhsT=ks_codes[:, block(t)].bitcast(FP8X4),
+                    lhsT_scale=ks_scales[:, block(t)],
+                    rhs=es_codes[:, block(j)].bitcast(FP8X4),
+                    rhs_scale=es_scales[:, block(j)],
+                    start=True,
+                    stop=True,
+                )
+            return y
+
+        def store_floats(j, y, copy):
+            y_sb = keep.tile([P, PACK, P], F32, name="y_sb%d" % j)
+            copy(out=y_sb[:], in_=y[:])
+            nc.sync.dma_start(y_rows[:, :, block(j)], y_sb[:])
+
+        def round_y(j, y):
+            nc.scalar.copy(out=y_bf[:, block(j), :], in_=y[:].rearrange("p t e -> p e t"))
+
+        def store_words(j, n, codes):
+            quantize(codes[:], y_scales[:, block(j, n)], y_bf[:, block(j, n), :])
+            nc.sync.dma_start(word_rows[:, block(j, n)], codes[:].bitcast(I32))
+
+        turned_keys = []
+        for t in range(PACK):
+            gather_dealt(listed_keys[:, t, :], key_pool[t])
+            turned_keys.append(turn_keys(t))
+            if 0 < t < PACK - 1:
+                ks_bf = on_window(t, 0, [P, P, PACK], BF16, "ks_bf%d" % (t - 1))
+                scale_ks(turned_keys[t - 1], ks_bf[:])
+                quantize_ks(t - 1, 1, ks_bf[:])
+        split = KEY_CAST_ON_VECTOR
+        nc.vector.tensor_copy(*interleaved(key_bf[:, :split, :], listed_keys[:, :, :split]))
+        nc.scalar.copy(*interleaved(key_bf[:, split:, :], listed_keys[:, :, split:]))
+        ks_bf = on_window(PACK - 1, 0, [P, 2 * P, PACK], BF16, "ks_bf23")
+        scale_ks(turned_keys[2], ks_bf[:, block(0), :])
+        scale_ks(turned_keys[3], ks_bf[:, block(1), :])
+        quantize(key_codes[:], key_scales[:], key_bf[:])
+        quantize_ks(2, 2, ks_bf[:])
+
+        err = [psum.tile([P, PACK, P], F32, name="err%d" % j) for j in range(E // P)]
+        state_codes = [
+            keep.tile([P, 2 * P], U32, name="state_codes0", align_bytes=64),
+            on_window(PACK, 2048, [P, 2 * P], U32, "state_codes1"),
+        ]
+        cast_state(0, 2)
+        quantize_state(0, 2, state_codes[0][:])
+        cast_state(2, 2)
+        minus_b = [predict(0, state_codes[0]), predict(1, state_codes[0])]
+
+        turn_into(err[0], gather_vals(0), True, False)
+        quantize_state(2, 2, state_codes[1][:])
+        turn_into(err[0], minus_b[0], False, True)
+        turn_into(err[1], minus_b[1], True, False)
+        minus_b = minus_b + [predict(2, state_codes[1]), predict(3, state_codes[1])]
+
+        turn_into(err[1], gather_vals(1), False, True)
+        make_es(0, err[0], on_window(PACK + 1, 0, [P, P, PACK], BF16, "es_bf0"))
+        turn_into(err[2], minus_b[2], True, False)
+        turn_into(err[3], minus_b[3], True, False)
+        y0 = update(0)
+        store_floats(0, y0, nc.scalar.copy)
+        round_y(0, y0)
+
+        turn_into(err[2], gather_vals(2), False, True)
+        make_es(1, err[1], on_window(PACK + 2, 0, [P, P, PACK], BF16, "es_bf1"))
+        y1 = update(1)
+        store_floats(1, y1, nc.scalar.copy)
+        round_y(1, y1)
+
+        turn_into(err[3], gather_vals(3), False, True)
+        make_es(2, err[2], on_window(PACK + 3, 0, [P, P, PACK], BF16, "es_bf2"))
+        y2 = update(2)
+        round_y(2, y2)
+        make_es(3, err[3], on_window(PACK + 3, 1024, [P, P, PACK], BF16, "es_bf3"))
+        y3 = update(3)
+        round_y(3, y3)
+        store_words(0, 2, on_window(PACK + 3, 2048, [P, 2 * P], U32, "y_codes01"))
+        store_words(2, 1, on_window(PACK + 3, 3072, [P, P], U32, "y_codes2"))
+        store_floats(2, y2, nc.vector.tensor_copy)
+        store_words(3, 1, on_window(PACK + 3, 3584, [P, P], U32, "y_codes3"))
+        store_floats(3, y3, nc.scalar.copy)
+
+        for q in range(4):
+            queue = nc.sync if q % 2 == 0 else nc.scalar
+            queue.dma_start(scale_rows[4 * q : 4 * q + 4, :], y_scales[32 * q : 32 * q + 4, :].bitcast(I32))

@@ -19,7 +19,7 @@ COPY = mybir.ActivationFunctionType.Copy
 P = 128
 PACK = 4
 WINDOW_BYTES = 4 * T
-KEY_CAST_ON_VECTOR = 256
+KEY_CAST_ON_VECTOR = 320
 
 
 def block(j, n=1):
@@ -41,16 +41,22 @@ def tile_attend_deltastep_pl_kernel(tc, state, keys, vals, step, vsc, dsc, offs,
         val_pool = [on_window(PACK + j, 0, [P, T], F32, "val_pool%d" % j) for j in range(E // P)]
         state_raw = keep.tile([P, PACK, E], F32, name="state_raw")
         dsc_sb = keep.tile([P, PACK], F32, name="dsc_sb")
-        step_sb = keep.tile([P, PACK], F32, name="step_sb")
-        vsc_sb = keep.tile([P, PACK], F32, name="vsc_sb")
+        slot_rows = keep.tile([P, P], F32, name="slot_rows")
+        slot_scales = keep.tile([P, 2 * PACK], F32, name="slot_scales")
+        step_sb = slot_scales[:, :PACK]
+        vsc_sb = slot_scales[:, PACK:]
         ident = keep.tile([P, P], F32, name="ident")
 
         key_planes = keys.rearrange("(p t) n -> p t n", t=PACK)
         nc.sync.dma_start(key_pool[0][:], key_planes[:, 0, :])
         nc.sync.dma_start(offsets[:], offs)
         nc.scalar.dma_start(dsc_sb[:], dsc.rearrange("o (p t) -> p (o t)", t=PACK))
-        nc.scalar.dma_start(step_sb[:], step.rearrange("(s r) o -> s (r o)", r=PACK))
-        nc.scalar.dma_start(vsc_sb[:], vsc.rearrange("(s r) o -> s (r o)", r=PACK))
+        nc.vector.memset(slot_rows[:], 0.0)
+        for first, column in ((0, step), (PACK, vsc)):
+            nc.sync.dma_start(
+                slot_rows[first : first + PACK, :].rearrange("r (q u) -> r q u", u=8),
+                column.rearrange("(q r u) o -> r q (u o)", r=PACK, u=8),
+            )
         for t in range(1, PACK):
             nc.sync.dma_start(key_pool[t][:], key_planes[:, t, :])
         nc.sync.dma_start(state_raw[:], state.rearrange("(p t) e -> p t e", t=PACK))
@@ -60,7 +66,7 @@ def tile_attend_deltastep_pl_kernel(tc, state, keys, vals, step, vsc, dsc, offs,
 
         def gather_dealt(dst, window):
             nc.vector.tensor_copy(
-                out=dst.bitcast(U32).rearrange("p (r s) -> p s r", r=PACK),
+                out=dst.bitcast(U32).rearrange("p (r q u) -> p q r u", r=PACK, u=8),
                 in_=window[:].bitcast(U32).indirect(offsets[:]),
             )
 
@@ -68,7 +74,7 @@ def tile_attend_deltastep_pl_kernel(tc, state, keys, vals, step, vsc, dsc, offs,
             nc.vector.quantize_mx(out=codes.bitcast(FP8X4), scales=scales, in_=grouped.rearrange("p c t -> p (c t)"))
 
         def per_slot(scale_sb):
-            return scale_sb[:].unsqueeze(1).to_broadcast([P, P, PACK])
+            return scale_sb.unsqueeze(1).to_broadcast([P, P, PACK])
 
         def interleaved(dst, src):
             return (
@@ -88,14 +94,12 @@ def tile_attend_deltastep_pl_kernel(tc, state, keys, vals, step, vsc, dsc, offs,
                 )
 
         listed_keys = keep.tile([P, PACK, I], F32, name="listed_keys")
-        ks_codes = keep.tile([P, D], U32, name="ks_codes", align_bytes=64)
         ks_scales = keep.tile([P, D], U8, name="ks_scales", align_bytes=64)
         key_bf = keep.tile([P, I, PACK], BF16, name="key_bf", align_bytes=64)
         key_codes = keep.tile([P, I], U32, name="key_codes", align_bytes=64)
         key_scales = keep.tile([P, I], U8, name="key_scales", align_bytes=64)
         state_bf = keep.tile([P, E, PACK], BF16, name="state_bf", align_bytes=64)
         state_scales = keep.tile([P, E], U8, name="state_scales", align_bytes=64)
-        es_codes = keep.tile([P, E], U32, name="es_codes", align_bytes=64)
         es_scales = keep.tile([P, E], U8, name="es_scales", align_bytes=64)
         y_bf = keep.tile([P, E, PACK], BF16, name="y_bf", align_bytes=64)
         y_scales = keep.tile([P, E], U8, name="y_scales", align_bytes=64)
@@ -114,7 +118,7 @@ def tile_attend_deltastep_pl_kernel(tc, state, keys, vals, step, vsc, dsc, offs,
             nc.vector.tensor_tensor(out=ks_bf, in0=turned[:].rearrange("s r p -> s p r"), in1=per_slot(step_sb), op=MULT)
 
         def quantize_ks(t, n, ks_bf):
-            quantize(ks_codes[:, block(t, n)], ks_scales[:, block(t, n)], ks_bf)
+            quantize(ks_codes[min(t, 2)][:], ks_scales[:, block(t, n)], ks_bf)
 
         def gather_vals(j):
             listed_vals = keep.tile([P, I], F32, name="listed_vals%d" % j)
@@ -130,7 +134,7 @@ def tile_attend_deltastep_pl_kernel(tc, state, keys, vals, step, vsc, dsc, offs,
             quantize(codes, state_scales[:, cols], state_bf[:, cols, :])
 
         def predict(j, codes):
-            b = psum.tile([P, I], F32, name="b", tag="work", bufs=2)
+            b = psum.tile([P, I], F32, name="b", tag="y" if j < 2 else "work", bufs=2)
             nc.tensor.matmul_mx(
                 out=b[:],
                 lhsT=codes[:, block(j % 2)].bitcast(FP8X4),
@@ -144,95 +148,119 @@ def tile_attend_deltastep_pl_kernel(tc, state, keys, vals, step, vsc, dsc, offs,
             nc.scalar.activation(out=minus_b[:], in_=b[:], func=COPY, scale=-1.0)
             return minus_b
 
-        def make_es(j, err, es_bf):
+        def make_es(err, es_bf):
             nc.vector.tensor_tensor(out=es_bf[:], in0=err[:].rearrange("s r e -> s e r"), in1=per_slot(vsc_sb), op=MULT)
-            quantize(es_codes[:, block(j)], es_scales[:, block(j)], es_bf[:])
+            return es_bf
 
-        def update(j):
-            y = psum.tile([P, PACK, P], F32, name="y", tag="y", bufs=2)
-            for t in range(PACK):
-                nc.tensor.matmul_mx(
-                    out=y[:, t, :],
-                    lhsT=ks_codes[:, block(t)].bitcast(FP8X4),
-                    lhsT_scale=ks_scales[:, block(t)],
-                    rhs=es_codes[:, block(j)].bitcast(FP8X4),
-                    rhs_scale=es_scales[:, block(j)],
-                    start=True,
-                    stop=True,
-                )
-            return y
+        def update(j, es_bf, es_codes, tags):
+            quantize(es_codes[:], es_scales[:, block(j)], es_bf[:])
+            n = PACK // len(tags)
+            banks = []
+            for tag in tags:
+                y = psum.tile([P, n, P], F32, name="y", tag=tag, bufs=2 if tag in ("y", "work") else 1)
+                for t in range(n):
+                    nc.tensor.matmul_mx(
+                        out=y[:, t, :],
+                        lhsT=ks_codes[min(n * len(banks) + t, 2)][:, block(max(n * len(banks) + t - 2, 0))].bitcast(FP8X4),
+                        lhsT_scale=ks_scales[:, block(n * len(banks) + t)],
+                        rhs=es_codes[:].bitcast(FP8X4),
+                        rhs_scale=es_scales[:, block(j)],
+                        start=True,
+                        stop=True,
+                    )
+                banks.append(y)
+            return banks
 
-        def store_floats(j, y, copy):
+        def store_floats(j, banks, copies, queues):
             y_sb = keep.tile([P, PACK, P], F32, name="y_sb%d" % j)
-            copy(out=y_sb[:], in_=y[:])
-            nc.sync.dma_start(y_rows[:, :, block(j)], y_sb[:])
+            n = PACK // len(banks)
+            for h in range(len(banks)):
+                rows = slice(n * h, n * (h + 1))
+                copies[h](out=y_sb[:, rows, :], in_=banks[h][:])
+            queues[0].dma_start(y_rows[:, :, block(j)], y_sb[:])
+            return y_sb
 
-        def round_y(j, y):
-            nc.scalar.copy(out=y_bf[:, block(j), :], in_=y[:].rearrange("p t e -> p e t"))
+        def round_from_bank(j, banks):
+            nc.scalar.copy(out=y_bf[:, block(j), :], in_=banks[0][:].rearrange("p t e -> p e t"))
+
+        def round_from_sbuf(j, y_sb):
+            nc.vector.tensor_copy(*interleaved(y_bf[:, block(j), :], y_sb[:]))
 
         def store_words(j, n, codes):
             quantize(codes[:], y_scales[:, block(j, n)], y_bf[:, block(j, n), :])
             nc.sync.dma_start(word_rows[:, block(j, n)], codes[:].bitcast(I32))
 
+        slot_columns = psum.tile([P, P], F32, name="slot_columns", tag="y", bufs=2)
+        nc.tensor.transpose(slot_columns[:], slot_rows[:], ident[:])
+        nc.scalar.copy(out=slot_scales[:], in_=slot_columns[:, : 2 * PACK])
+
         turned_keys = []
+        ks_codes = [
+            on_window(2, 4096, [P, P], U32, "ks_codes0"),
+            on_window(3, 4096, [P, P], U32, "ks_codes1"),
+            on_window(PACK, 4096, [P, 2 * P], U32, "ks_codes23"),
+        ]
+        ks_bf = [on_window(t + 1, 0, [P, P, PACK], BF16, "ks_bf%d" % t) for t in range(2)]
         for t in range(PACK):
             gather_dealt(listed_keys[:, t, :], key_pool[t])
             turned_keys.append(turn_keys(t))
             if 0 < t < PACK - 1:
-                ks_bf = on_window(t, 0, [P, P, PACK], BF16, "ks_bf%d" % (t - 1))
-                scale_ks(turned_keys[t - 1], ks_bf[:])
-                quantize_ks(t - 1, 1, ks_bf[:])
+                scale_ks(turned_keys[t - 1], ks_bf[t - 1][:])
+            if t == 2:
+                quantize_ks(0, 1, ks_bf[0][:])
         split = KEY_CAST_ON_VECTOR
         nc.vector.tensor_copy(*interleaved(key_bf[:, :split, :], listed_keys[:, :, :split]))
         nc.scalar.copy(*interleaved(key_bf[:, split:, :], listed_keys[:, :, split:]))
-        ks_bf = on_window(PACK - 1, 0, [P, 2 * P, PACK], BF16, "ks_bf23")
-        scale_ks(turned_keys[2], ks_bf[:, block(0), :])
-        scale_ks(turned_keys[3], ks_bf[:, block(1), :])
+        ks_bf23 = on_window(PACK - 1, 0, [P, 2 * P, PACK], BF16, "ks_bf23")
+        scale_ks(turned_keys[2], ks_bf23[:, block(0), :])
+        quantize_ks(1, 1, ks_bf[1][:])
         quantize(key_codes[:], key_scales[:], key_bf[:])
-        quantize_ks(2, 2, ks_bf[:])
+        scale_ks(turned_keys[3], ks_bf23[:, block(1), :])
 
-        err = [psum.tile([P, PACK, P], F32, name="err%d" % j) for j in range(E // P)]
+        err = [psum.tile([P, PACK, P], F32, name="err", tag="err%d" % (j % 2)) for j in range(E // P)]
         state_codes = [
             keep.tile([P, 2 * P], U32, name="state_codes0", align_bytes=64),
-            on_window(PACK, 2048, [P, 2 * P], U32, "state_codes1"),
+            on_window(PACK + 0, 2048, [P, 2 * P], U32, "state_codes1"),
         ]
-        cast_state(0, 2)
-        quantize_state(0, 2, state_codes[0][:])
+        for j in range(2):
+            cast_state(j, 1)
+            quantize_state(j, 1, state_codes[0][:, block(j)])
         cast_state(2, 2)
         minus_b = [predict(0, state_codes[0]), predict(1, state_codes[0])]
 
-        turn_into(err[0], gather_vals(0), True, False)
+        listed = gather_vals(0)
         quantize_state(2, 2, state_codes[1][:])
+        quantize_ks(2, 2, ks_bf23[:])
+        turn_into(err[0], listed, True, False)
         turn_into(err[0], minus_b[0], False, True)
         turn_into(err[1], minus_b[1], True, False)
         minus_b = minus_b + [predict(2, state_codes[1]), predict(3, state_codes[1])]
 
         turn_into(err[1], gather_vals(1), False, True)
-        make_es(0, err[0], on_window(PACK + 1, 0, [P, P, PACK], BF16, "es_bf0"))
+        es0 = make_es(err[0], on_window(PACK + 1, 0, [P, P, PACK], BF16, "es_bf0"))
+        y0 = update(0, es0, on_window(PACK + 1, 1024, [P, P], U32, "es_codes0"), ["y"])
         turn_into(err[2], minus_b[2], True, False)
-        turn_into(err[3], minus_b[3], True, False)
-        y0 = update(0)
-        store_floats(0, y0, nc.scalar.copy)
-        round_y(0, y0)
+        store_floats(0, y0, [nc.scalar.copy], [nc.sync])
+        round_from_bank(0, y0)
 
         turn_into(err[2], gather_vals(2), False, True)
-        make_es(1, err[1], on_window(PACK + 2, 0, [P, P, PACK], BF16, "es_bf1"))
-        y1 = update(1)
-        store_floats(1, y1, nc.scalar.copy)
-        round_y(1, y1)
+        es1 = make_es(err[1], on_window(PACK + 2, 0, [P, P, PACK], BF16, "es_bf1"))
+        turn_into(err[3], minus_b[3], True, False)
 
         turn_into(err[3], gather_vals(3), False, True)
-        make_es(2, err[2], on_window(PACK + 3, 0, [P, P, PACK], BF16, "es_bf2"))
-        y2 = update(2)
-        round_y(2, y2)
-        make_es(3, err[3], on_window(PACK + 3, 1024, [P, P, PACK], BF16, "es_bf3"))
-        y3 = update(3)
-        round_y(3, y3)
-        store_words(0, 2, on_window(PACK + 3, 2048, [P, 2 * P], U32, "y_codes01"))
-        store_words(2, 1, on_window(PACK + 3, 3072, [P, P], U32, "y_codes2"))
-        store_floats(2, y2, nc.vector.tensor_copy)
-        store_words(3, 1, on_window(PACK + 3, 3584, [P, P], U32, "y_codes3"))
-        store_floats(3, y3, nc.scalar.copy)
+        es2 = make_es(err[2], on_window(PACK + 3, 0, [P, P, PACK], BF16, "es_bf2"))
+        y1 = update(1, es1, on_window(PACK + 2, 4096, [P, P], U32, "es_codes1"), ["y"])
+        y2 = update(2, es2, on_window(PACK + 3, 4608, [P, P], U32, "es_codes2"), ["work"])
+        es3 = make_es(err[3], on_window(PACK + 3, 1024, [P, P, PACK], BF16, "es_bf3"))
+        y3 = update(3, es3, on_window(PACK + 3, 5120, [P, P], U32, "es_codes3"), ["y_low", "y_high"])
+        y_sb1 = store_floats(1, y1, [nc.scalar.copy], [nc.sync])
+        round_from_bank(1, y1)
+        y_sb2 = store_floats(2, y2, [nc.scalar.copy], [nc.sync])
+        y_sb3 = store_floats(3, y3, [nc.vector.tensor_copy, nc.scalar.copy], [nc.scalar])
+        store_words(0, 2, on_window(PACK + 3, 1024, [P, 2 * P], U32, "y_codes01"))
+        round_from_sbuf(2, y_sb2)
+        round_from_sbuf(3, y_sb3)
+        store_words(2, 2, on_window(PACK + 3, 3072, [P, 2 * P], U32, "y_codes23"))
 
         for q in range(4):
             queue = nc.sync if q % 2 == 0 else nc.scalar

from contextlib import ExitStack

import concourse.mybir as mybir
from concourse.masks import make_identity

D, T, I, E = 512, 2048, 512, 512
FLOPS = 2 * D * I * E + 2 * I * D * E

F32 = mybir.dt.float32
BF16 = mybir.dt.bfloat16
I32 = mybir.dt.int32
U32 = mybir.dt.uint32
U16 = mybir.dt.uint16
U8 = mybir.dt.uint8
FP8X4 = mybir.dt.float8_e4m3fn_x4
MULT = mybir.AluOpType.mult
COPY = mybir.ActivationFunctionType.Copy

P = 128
PACK = 4
WINDOW_BYTES = 4 * T
KEY_CAST_ON_VECTOR = 320


def block(j, n=1):
    return slice(j * P, (j + n) * P)


def tile_attend_deltastep_pl_kernel(tc, state, keys, vals, step, vsc, dsc, offs, out_0, out_1, out_2):
    nc = tc.nc
    with ExitStack() as ctx:
        keep = ctx.enter_context(tc.tile_pool(name="keep", bufs=1))
        windows = ctx.enter_context(tc.tile_pool(name="windows", bufs=1))
        psum = ctx.enter_context(tc.psum_pool(name="psum", bufs=1))

        def on_window(w, at, shape, dtype, name):
            return windows.tile(shape, dtype, name=name, offset=w * WINDOW_BYTES + at, align_bytes=64)

        offsets = keep.tile([P, I // 16], U16, name="offsets")
        key_pool = [on_window(t, 0, [P, T], F32, "key_pool%d" % t) for t in range(PACK)]
        val_pool = [on_window(PACK + j, 0, [P, T], F32, "val_pool%d" % j) for j in range(E // P)]
        state_raw = keep.tile([P, PACK, E], F32, name="state_raw")
        dsc_sb = keep.tile([P, PACK], F32, name="dsc_sb")
        slot_rows = keep.tile([P, P], F32, name="slot_rows")
        slot_scales = keep.tile([P, 2 * PACK], F32, name="slot_scales")
        step_sb = slot_scales[:, :PACK]
        vsc_sb = slot_scales[:, PACK:]
        ident = keep.tile([P, P], F32, name="ident")

        key_planes = keys.rearrange("(p t) n -> p t n", t=PACK)
        nc.sync.dma_start(key_pool[0][:], key_planes[:, 0, :])
        nc.sync.dma_start(offsets[:], offs)
        nc.scalar.dma_start(dsc_sb[:], dsc.rearrange("o (p t) -> p (o t)", t=PACK))
        nc.vector.memset(slot_rows[:], 0.0)
        for first, column in ((0, step), (PACK, vsc)):
            nc.sync.dma_start(
                slot_rows[first : first + PACK, :].rearrange("r (q u) -> r q u", u=8),
                column.rearrange("(q r u) o -> r q (u o)", r=PACK, u=8),
            )
        for t in range(1, PACK):
            nc.sync.dma_start(key_pool[t][:], key_planes[:, t, :])
        nc.sync.dma_start(state_raw[:], state.rearrange("(p t) e -> p t e", t=PACK))
        for j in range(E // P):
            nc.sync.dma_start(val_pool[j][:], vals[block(j), :])
        make_identity(nc, ident[:])

        def gather_dealt(dst, window):
            nc.vector.tensor_copy(
                out=dst.bitcast(U32).rearrange("p (r q u) -> p q r u", r=PACK, u=8),
                in_=window[:].bitcast(U32).indirect(offsets[:]),
            )

        def quantize(codes, scales, grouped):
            nc.vector.quantize_mx(out=codes.bitcast(FP8X4), scales=scales, in_=grouped.rearrange("p c t -> p (c t)"))

        def per_slot(scale_sb):
            return scale_sb.unsqueeze(1).to_broadcast([P, P, PACK])

        def interleaved(dst, src):
            return (
                dst.rearrange("p (c i) t -> p c t i", i=4),
                src.rearrange("p t (c i) -> p c t i", i=4),
            )

        def turn_into(bank, src, start, stop):
            for r in range(PACK):
                nc.tensor.matmul(
                    bank[:, r, :],
                    src[:, block(r)],
                    ident[:],
                    start=start and r == 0,
                    stop=stop and r == PACK - 1,
                    is_transpose=True,
                )

        listed_keys = keep.tile([P, PACK, I], F32, name="listed_keys")
        ks_scales = keep.tile([P, D], U8, name="ks_scales", align_bytes=64)
        key_bf = keep.tile([P, I, PACK], BF16, name="key_bf", align_bytes=64)
        key_codes = keep.tile([P, I], U32, name="key_codes", align_bytes=64)
        key_scales = keep.tile([P, I], U8, name="key_scales", align_bytes=64)
        state_bf = keep.tile([P, E, PACK], BF16, name="state_bf", align_bytes=64)
        state_scales = keep.tile([P, E], U8, name="state_scales", align_bytes=64)
        es_scales = keep.tile([P, E], U8, name="es_scales", align_bytes=64)
        y_bf = keep.tile([P, E, PACK], BF16, name="y_bf", align_bytes=64)
        y_scales = keep.tile([P, E], U8, name="y_scales", align_bytes=64)
        y_rows = out_0.rearrange("(p t) e -> p t e", t=PACK)
        word_rows = out_1.rearrange("z p c r -> p (z c r)").bitcast(I32)
        scale_rows = out_2.rearrange("z q c -> q (z c)").bitcast(I32)

        def turn_keys(t):
            kd = keep.tile([P, I], F32, name="kd%d" % t)
            nc.scalar.activation(out=kd[:], in_=listed_keys[:, t, :], func=COPY, scale=dsc_sb[:, t : t + 1])
            turned = psum.tile([P, PACK, P], F32, name="turned", tag="work", bufs=2)
            turn_into(turned, kd, True, True)
            return turned

        def scale_ks(turned, ks_bf):
            nc.vector.tensor_tensor(out=ks_bf, in0=turned[:].rearrange("s r p -> s p r"), in1=per_slot(step_sb), op=MULT)

        def quantize_ks(t, n, ks_bf):
            quantize(ks_codes[min(t, 2)][:], ks_scales[:, block(t, n)], ks_bf)

        def gather_vals(j):
            listed_vals = keep.tile([P, I], F32, name="listed_vals%d" % j)
            gather_dealt(listed_vals[:], val_pool[j])
            return listed_vals

        def cast_state(j, n):
            cols = block(j, n)
            nc.scalar.copy(*interleaved(state_bf[:, cols, :], state_raw[:, :, cols]))

        def quantize_state(j, n, codes):
            cols = block(j, n)
            quantize(codes, state_scales[:, cols], state_bf[:, cols, :])

        def predict(j, codes):
            b = psum.tile([P, I], F32, name="b", tag="y" if j < 2 else "work", bufs=2)
            nc.tensor.matmul_mx(
                out=b[:],
                lhsT=codes[:, block(j % 2)].bitcast(FP8X4),
                lhsT_scale=state_scales[:, block(j)],
                rhs=key_codes[:].bitcast(FP8X4),
                rhs_scale=key_scales[:],
                start=True,
                stop=True,
            )
            minus_b = keep.tile([P, I], F32, name="minus_b%d" % j)
            nc.scalar.activation(out=minus_b[:], in_=b[:], func=COPY, scale=-1.0)
            return minus_b

        def make_es(err, es_bf):
            nc.vector.tensor_tensor(out=es_bf[:], in0=err[:].rearrange("s r e -> s e r"), in1=per_slot(vsc_sb), op=MULT)
            return es_bf

        def update(j, es_bf, es_codes, tags):
            quantize(es_codes[:], es_scales[:, block(j)], es_bf[:])
            n = PACK // len(tags)
            banks = []
            for tag in tags:
                y = psum.tile([P, n, P], F32, name="y", tag=tag, bufs=2 if tag in ("y", "work") else 1)
                for t in range(n):
                    nc.tensor.matmul_mx(
                        out=y[:, t, :],
                        lhsT=ks_codes[min(n * len(banks) + t, 2)][:, block(max(n * len(banks) + t - 2, 0))].bitcast(FP8X4),
                        lhsT_scale=ks_scales[:, block(n * len(banks) + t)],
                        rhs=es_codes[:].bitcast(FP8X4),
                        rhs_scale=es_scales[:, block(j)],
                        start=True,
                        stop=True,
                    )
                banks.append(y)
            return banks

        def store_floats(j, banks, copies, queues):
            y_sb = keep.tile([P, PACK, P], F32, name="y_sb%d" % j)
            n = PACK // len(banks)
            for h in range(len(banks)):
                rows = slice(n * h, n * (h + 1))
                copies[h](out=y_sb[:, rows, :], in_=banks[h][:])
            queues[0].dma_start(y_rows[:, :, block(j)], y_sb[:])
            return y_sb

        def round_from_bank(j, banks):
            nc.scalar.copy(out=y_bf[:, block(j), :], in_=banks[0][:].rearrange("p t e -> p e t"))

        def round_from_sbuf(j, y_sb):
            nc.vector.tensor_copy(*interleaved(y_bf[:, block(j), :], y_sb[:]))

        def store_words(j, n, codes):
            quantize(codes[:], y_scales[:, block(j, n)], y_bf[:, block(j, n), :])
            nc.sync.dma_start(word_rows[:, block(j, n)], codes[:].bitcast(I32))

        slot_columns = psum.tile([P, P], F32, name="slot_columns", tag="y", bufs=2)
        nc.tensor.transpose(slot_columns[:], slot_rows[:], ident[:])
        nc.scalar.copy(out=slot_scales[:], in_=slot_columns[:, : 2 * PACK])

        turned_keys = []
        ks_codes = [
            on_window(2, 4096, [P, P], U32, "ks_codes0"),
            on_window(3, 4096, [P, P], U32, "ks_codes1"),
            on_window(PACK, 4096, [P, 2 * P], U32, "ks_codes23"),
        ]
        ks_bf = [on_window(t + 1, 0, [P, P, PACK], BF16, "ks_bf%d" % t) for t in range(2)]
        for t in range(PACK):
            gather_dealt(listed_keys[:, t, :], key_pool[t])
            turned_keys.append(turn_keys(t))
            if 0 < t < PACK - 1:
                scale_ks(turned_keys[t - 1], ks_bf[t - 1][:])
            if t == 2:
                quantize_ks(0, 1, ks_bf[0][:])
        split = KEY_CAST_ON_VECTOR
        nc.vector.tensor_copy(*interleaved(key_bf[:, :split, :], listed_keys[:, :, :split]))
        nc.scalar.copy(*interleaved(key_bf[:, split:, :], listed_keys[:, :, split:]))
        ks_bf23 = on_window(PACK - 1, 0, [P, 2 * P, PACK], BF16, "ks_bf23")
        scale_ks(turned_keys[2], ks_bf23[:, block(0), :])
        quantize_ks(1, 1, ks_bf[1][:])
        quantize(key_codes[:], key_scales[:], key_bf[:])
        scale_ks(turned_keys[3], ks_bf23[:, block(1), :])

        err = [psum.tile([P, PACK, P], F32, name="err", tag="err%d" % (j % 2)) for j in range(E // P)]
        state_codes = [
            keep.tile([P, 2 * P], U32, name="state_codes0", align_bytes=64),
            on_window(PACK + 0, 2048, [P, 2 * P], U32, "state_codes1"),
        ]
        for j in range(2):
            cast_state(j, 1)
            quantize_state(j, 1, state_codes[0][:, block(j)])
        cast_state(2, 2)
        minus_b = [predict(0, state_codes[0]), predict(1, state_codes[0])]

        listed = gather_vals(0)
        quantize_state(2, 2, state_codes[1][:])
        quantize_ks(2, 2, ks_bf23[:])
        turn_into(err[0], listed, True, False)
        turn_into(err[0], minus_b[0], False, True)
        turn_into(err[1], minus_b[1], True, False)
        minus_b = minus_b + [predict(2, state_codes[1]), predict(3, state_codes[1])]

        turn_into(err[1], gather_vals(1), False, True)
        es0 = make_es(err[0], on_window(PACK + 1, 0, [P, P, PACK], BF16, "es_bf0"))
        y0 = update(0, es0, on_window(PACK + 1, 1024, [P, P], U32, "es_codes0"), ["y"])
        turn_into(err[2], minus_b[2], True, False)
        store_floats(0, y0, [nc.scalar.copy], [nc.sync])
        round_from_bank(0, y0)

        turn_into(err[2], gather_vals(2), False, True)
        es1 = make_es(err[1], on_window(PACK + 2, 0, [P, P, PACK], BF16, "es_bf1"))
        turn_into(err[3], minus_b[3], True, False)

        turn_into(err[3], gather_vals(3), False, True)
        es2 = make_es(err[2], on_window(PACK + 3, 0, [P, P, PACK], BF16, "es_bf2"))
        y1 = update(1, es1, on_window(PACK + 2, 4096, [P, P], U32, "es_codes1"), ["y"])
        y2 = update(2, es2, on_window(PACK + 3, 4608, [P, P], U32, "es_codes2"), ["work"])
        es3 = make_es(err[3], on_window(PACK + 3, 1024, [P, P, PACK], BF16, "es_bf3"))
        y3 = update(3, es3, on_window(PACK + 3, 5120, [P, P], U32, "es_codes3"), ["y_low", "y_high"])
        y_sb1 = store_floats(1, y1, [nc.scalar.copy], [nc.sync])
        round_from_bank(1, y1)
        y_sb2 = store_floats(2, y2, [nc.scalar.copy], [nc.sync])
        y_sb3 = store_floats(3, y3, [nc.vector.tensor_copy, nc.scalar.copy], [nc.scalar])
        store_words(0, 2, on_window(PACK + 3, 1024, [P, 2 * P], U32, "y_codes01"))
        round_from_sbuf(2, y_sb2)
        round_from_sbuf(3, y_sb3)
        store_words(2, 2, on_window(PACK + 3, 3072, [P, 2 * P], U32, "y_codes23"))

        for q in range(4):
            queue = nc.sync if q % 2 == 0 else nc.scalar
            queue.dma_start(scale_rows[4 * q : 4 * q + 4, :], y_scales[32 * q : 32 * q + 4, :].bitcast(I32))
